import numpy as np
import ml_dtypes


def mxq(x, axis, fmt="e4m3"):
    dtype, down = {"e4m3": (ml_dtypes.float8_e4m3fn, 7), "e5m2": (ml_dtypes.float8_e5m2, 14)}[fmt]
    v = np.moveaxis(np.asarray(x, np.float32).astype(ml_dtypes.bfloat16).astype(np.float64), axis, -1)
    blocks = v.reshape(v.shape[:-1] + (-1, 32))
    amax = np.abs(blocks).max(-1, keepdims=True)
    byte = np.maximum(np.where(amax > 0, np.frexp(amax)[1] - 1 + 127, 0) - down, 1)
    scale = np.exp2(byte - 127.0)
    codes = (blocks / scale).astype(np.float32).astype(dtype).astype(np.float64)
    return np.moveaxis((codes * scale).reshape(v.shape), -1, axis)


WIDE = False


def mx_kscale(k):
    if not WIDE:
        return np.ones(k)
    levels = np.array([10, -10, 5, -5, 0])
    if k % 512:
        return np.exp2(np.random.permutation(np.resize(levels, k // 32))).repeat(32)
    a = np.empty((k // 512, 16))
    for p in range(k // 512):
        a[p, :8] = np.random.permutation(np.resize(levels, 8))
        for g in range(8):
            far = levels[np.abs(levels - a[p, g]) >= 10]
            a[p, g + 8] = far[np.random.randint(len(far))]
    return np.exp2(a.ravel()).repeat(32)


def f64(x):
    return np.asarray(x).astype(np.float64)


def striped(idx):
    return np.tile(idx.reshape(-1, 16).T, (8, 1)).astype(np.uint16)


def unstriped(offs):
    return offs[:16].T.reshape(-1).astype(np.int64)


def pack_weight(w):
    k, n = w.shape
    w = f64(np.asarray(w, np.float32).astype(ml_dtypes.bfloat16)).reshape(k // 32, 32, n)
    amax = np.abs(w).max(1)
    byte = np.clip(np.where(amax > 0, np.frexp(amax)[1] - 1 + 127 - 7, 1), 1, 254)
    scaled = (w * np.exp2(127.0 - byte)[:, None, :]).reshape(k, n).astype(np.float32)
    words = np.ascontiguousarray(scaled.reshape(k // 512, 128, 4, n).transpose(0, 1, 3, 2)).astype(ml_dtypes.float8_e4m3fn).view(np.uint8)
    return words, np.ascontiguousarray(byte.astype(np.uint8).reshape(k // 512, 16, n))


def unpack_weight(words, scales):
    g, p, n, _ = words.shape
    vals = np.ascontiguousarray(words).view(ml_dtypes.float8_e4m3fn).astype(np.float64) * np.repeat(np.exp2(scales.astype(np.float64) - 127.0), 8, axis=1)[..., None]
    return vals.transpose(0, 1, 3, 2).reshape(g * 512, n)


def sigmoid(v):
    return 1.0 / (1.0 + np.exp(-np.maximum(v, -700.0)))


K, T, S, H, C = 512, 2048, 512, 512, 512


def setup_inputs():
    n = np.random.standard_normal
    s = mx_kscale(K)[:, None]
    packed_xT = pack_weight(n((K, T)) * s)
    return {
        "x_words": packed_xT[0],
        "x_scales": packed_xT[1],
        "w1": (n((K, H)) / np.sqrt(K) / s).astype(np.float32),
        "sl": np.random.uniform(1.0, 2.0, (H, 1)).astype(np.float32),
        "th": (0.5 * n((H, 1))).astype(np.float32),
        "gs": (np.random.uniform(0.5, 1.5, (K, 1)) / s).astype(np.float32),
        "gs2": (np.random.uniform(0.5, 1.5, (K, 1)) / s).astype(np.float32),
        "offs": striped(np.random.permutation(T)[:S]),
        "n1": striped(np.random.permutation(S)),
        "n2": striped(np.random.permutation(S)),
        "n3": striped(np.random.permutation(S)),
        "ca": striped(np.random.permutation(T)[:C]),
        "cb": striped(np.random.permutation(T)[:C]),
        "n4": striped(np.random.permutation(S)),
        "n5": striped(np.random.permutation(S)),
        "n6": striped(np.random.permutation(S)),
    }


def reference(x_words, x_scales, w1, sl, th, gs, gs2, offs, n1, n2, n3, ca, cb, n4, n5, n6):
    x_cb = unpack_weight(x_words, x_scales)[:, unstriped(cb)]
    xq = unpack_weight(x_words, x_scales)[:, unstriped(offs)]
    y = mxq(f64(w1), 0, "e4m3").T @ xq
    sg = sigmoid(f64(sl) * (y[:, unstriped(n3)] - f64(th)))
    z2 = f64(gs2) * (y * sg)
    b = 0.0625 * ((x_cb.T @ mxq(z2, 0, "e4m3")))
    x_ca = unpack_weight(x_words, x_scales)[:, unstriped(ca)]
    z = f64(gs) * (0.75 * ((y - y[:, unstriped(n1)]) * (y - y[:, unstriped(n2)])))
    a = 0.0625 * ((x_ca.T @ mxq(z, 0, "e4m3")))
    return b * (a[:, unstriped(n4)] - a) + 0.5 * (b[:, unstriped(n6)] * (a[:, unstriped(n5)] - a))

@@ -1,0 +1,180 @@
+from contextlib import ExitStack
+
+import concourse.mybir as mybir
+
+F32 = mybir.dt.float32
+BF16 = mybir.dt.bfloat16
+I32 = mybir.dt.int32
+U32 = mybir.dt.uint32
+U16 = mybir.dt.uint16
+U8 = mybir.dt.uint8
+FP8X4 = mybir.dt.float8_e4m3fn_x4
+MULT = mybir.AluOpType.mult
+ADD = mybir.AluOpType.add
+SUB = mybir.AluOpType.subtract
+COPY = mybir.ActivationFunctionType.Copy
+SIGMOID = mybir.ActivationFunctionType.Sigmoid
+
+P = 128
+PACK = 4
+T = 2048
+S = 512
+WIDE = 1024
+NARROW = 520
+FLOPS = 3 * 2 * 512 * 512 * 512
+
+
+def tile_picked_twocdflowbquadesa_none_p_kernel(tc, x_words, x_scales, w1, sl, th, gs, gs2, offs, n1, n2, n3, ca, cb, n4, n5, n6, out):
+    nc = tc.nc
+    with ExitStack() as ctx:
+        keep = ctx.enter_context(tc.tile_pool(name="keep", bufs=1))
+        ring = ctx.enter_context(tc.tile_pool(name="ring", bufs=3))
+        reuse = ctx.enter_context(tc.tile_pool(name="reuse", bufs=1))
+        psum = ctx.enter_context(tc.psum_pool(name="psum", bufs=1))
+
+        def load_list(src, name):
+            tile = keep.tile([P, S // 16], U16, name=name)
+            nc.sync.dma_start(out=tile[:], in_=src)
+            return tile
+
+        def load_rows(src, name):
+            tile = keep.tile([P, PACK], F32, name=name)
+            nc.gpsimd.dma_start(out=tile[:], in_=src.rearrange("(p t) o -> p (t o)", t=PACK))
+            return tile
+
+        xw = keep.tile([P, T], U32, name="xw", align_bytes=64)
+        xs = keep.tile([P, T], U8, name="xs", align_bytes=64)
+        nc.vector.memset(xs[:].bitcast(I32), 0)
+        nc.sync.dma_start(out=xw[:].bitcast(I32), in_=x_words[0].rearrange("p n t -> p (n t)").bitcast(I32))
+        l_offs = load_list(offs, "l_offs")
+        for q in range(4):
+            nc.sync.dma_start(out=xs[32 * q : 32 * q + 4, :].bitcast(I32), in_=x_scales[0, 4 * q : 4 * q + 4, :].bitcast(I32))
+        w_rows = w1.rearrange("(p j) c -> p j c", j=PACK)
+        w_raw = []
+        for h in range(2):
+            tile = keep.tile([P, PACK, 256], F32, name="w_raw%d" % h)
+            nc.sync.dma_start(out=tile[:], in_=w_rows[:, :, 256 * h : 256 * (h + 1)])
+            w_raw.append(tile)
+        l_ca = load_list(ca, "l_ca")
+        l_cb = load_list(cb, "l_cb")
+        l_n1 = load_list(n1, "l_n1")
+        l_n2 = load_list(n2, "l_n2")
+        l_n3 = load_list(n3, "l_n3")
+        l_n5 = load_list(n5, "l_n5")
+        l_n4 = load_list(n4, "l_n4")
+        l_n6 = load_list(n6, "l_n6")
+
+        gs_t = load_rows(gs, "gs_t")
+        gs2_t = load_rows(gs2, "gs2_t")
+        sl_t = load_rows(sl, "sl_t")
+        th_t = load_rows(th, "th_t")
+        zfac = keep.tile([P, PACK], F32, name="zfac")
+        nc.gpsimd.tensor_scalar(out=zfac[:], in0=gs_t[:], scalar1=0.75, scalar2=0.0, op0=MULT, op1=ADD)
+        nth = keep.tile([P, PACK], F32, name="nth")
+        nc.gpsimd.tensor_scalar(out=nth[:], in0=th_t[:], scalar1=-1.0, scalar2=0.0, op0=MULT, op1=ADD)
+        sbias = keep.tile([P, PACK], F32, name="sbias")
+        nc.gpsimd.tensor_tensor(out=sbias[:], in0=nth[:], in1=sl_t[:], op=MULT)
+
+        def window(name, width):
+            tile = keep.tile([P, width], F32, name=name, align_bytes=64)
+            nc.vector.memset(tile[:, S:], 0.0)
+            return tile
+
+        y_win = [window("y_win%d" % t, WIDE) for t in range(PACK)]
+        u_win = [window("u_win%d" % t, WIDE) for t in range(PACK)]
+        a_win = [window("a_win%d" % t, NARROW) for t in range(PACK)]
+        b_win = [window("b_win%d" % t, NARROW) for t in range(PACK)]
+
+        def mx_tiles(name):
+            words = keep.tile([P, S], U32, name=name + "_w", align_bytes=64)
+            scales = keep.tile([P, S], U8, name=name + "_s", align_bytes=64)
+            return words, scales
+
+        def pick(lst, words, scales):
+            nc.vector.tensor_copy(out=words[:], in_=xw[:].indirect(lst[:]))
+            nc.vector.tensor_copy(out=scales[:], in_=xs[:].indirect(lst[:]))
+            return words, scales
+
+        def quantize(grouped, name):
+            words = keep.tile([P, S], U32, name=name + "_w", align_bytes=64)
+            scales = keep.tile([P, S], U8, name=name + "_s", align_bytes=64)
+            nc.vector.quantize_mx(out=words[:].bitcast(FP8X4), scales=scales[:], in_=grouped[:])
+            return words, scales
+
+        def product(bank, stat, mov, i):
+            cols = slice(P * i, P * (i + 1))
+            nc.tensor.matmul_mx(out=bank[:], lhsT=stat[0][:, cols].bitcast(FP8X4), lhsT_scale=stat[1][:, cols],
+                                rhs=mov[0][:].bitcast(FP8X4), rhs_scale=mov[1][:], start=True, stop=True)
+
+        xq = pick(l_offs, *mx_tiles("xq"))
+
+        w_grp = reuse.tile([P, PACK * S], BF16, name="w_grp", align_bytes=64, offset=0)
+        w_view = w_grp[:].rearrange("p (t m j) -> p m t j", t=PACK, j=PACK)
+        for h in range(2):
+            nc.scalar.copy(out=w_view[:, 64 * h : 64 * (h + 1), :, :], in_=w_raw[h][:].rearrange("p j (m t) -> p m t j", t=PACK))
+        wq = mx_tiles("wq")
+        for h in range(2):
+            nc.vector.quantize_mx(out=wq[0][:, 256 * h : 256 * (h + 1)].bitcast(FP8X4), scales=wq[1][:, 256 * h : 256 * (h + 1)],
+                                  in_=w_grp[:, 1024 * h : 1024 * (h + 1)])
+        xca = pick(l_ca, *mx_tiles("xca"))
+        xcb_w = reuse.tile([P, S], U32, name="xcb_w", align_bytes=64, offset=0)
+        xcb_s = reuse.tile([P, S], U8, name="xcb_s", align_bytes=64, offset=2048)
+        xcb = pick(l_cb, xcb_w, xcb_s)
+
+        y_ps = [psum.tile([P, S], F32, name="y_ps%d" % t, tag="lo%d" % t) for t in range(PACK)]
+        u_dup = [keep.tile([P, S], F32, name="u_dup%d" % t) for t in range(PACK)]
+        g1 = [keep.tile([P, S], F32, name="g1_%d" % t) for t in range(PACK)]
+        d1 = keep.tile([P, PACK, S], F32, name="d1", align_bytes=64)
+        d2 = keep.tile([P, PACK, S], F32, name="d2", align_bytes=64)
+        ry = keep.tile([P, PACK, S], F32, name="ry", align_bytes=64)
+        sg = keep.tile([P, PACK, S], F32, name="sg", align_bytes=64)
+        for t in range(PACK):
+            product(y_ps[t], wq, xq, t)
+        for t in range(PACK):
+            nc.scalar.activation(out=u_win[t][:, :S], in_=y_ps[t][:], func=COPY, scale=zfac[:, t : t + 1])
+            nc.sync.dma_start(out=u_dup[t][:], in_=u_win[t][:, :S])
+        for t in range(PACK):
+            nc.vector.tensor_scalar(out=ry[:, t, :], in0=y_ps[t][:], scalar1=gs2_t[:, t : t + 1], scalar2=None, op0=MULT)
+        for t in range(PACK):
+            nc.scalar.copy(out=y_win[t][:, :S], in_=y_ps[t][:])
+            nc.scalar.activation(out=g1[t][:], in_=y_win[t][:].indirect(l_n1[:]), func=COPY)
+            nc.vector.tensor_tensor(out=d2[:, t, :], in0=u_win[t][:].indirect(l_n2[:]), in1=u_dup[t][:], op=SUB)
+            nc.vector.tensor_tensor(out=d1[:, t, :], in0=g1[t][:], in1=y_ps[t][:], op=SUB)
+
+        def weave(f0, f1, name):
+            grouped = keep.tile([P, PACK * S], BF16, name=name, tag="grouped", align_bytes=64)
+            nc.vector.tensor_tensor(out=grouped[:].rearrange("p (c i t) -> p c t i", i=2, t=PACK),
+                                    in0=f0[:].rearrange("p t (c i) -> p c t i", i=2),
+                                    in1=f1[:].rearrange("p t (c i) -> p c t i", i=2), op=MULT)
+            return grouped
+
+        zq = quantize(weave(d1, d2, "z_grp"), "zq")
+        a_ps = [psum.tile([P, S], F32, name="a_ps%d" % c, tag="hi%d" % c) for c in range(PACK)]
+        for c in range(PACK):
+            product(a_ps[c], xca, zq, c)
+        for t in range(PACK):
+            nc.scalar.activation(out=sg[:, t, :], in_=y_win[t][:].indirect(l_n3[:]), func=SIGMOID,
+                                 bias=sbias[:, t : t + 1], scale=sl_t[:, t : t + 1])
+        z2q = quantize(weave(ry, sg, "z2_grp"), "z2q")
+        b_ps = [psum.tile([P, S], F32, name="b_ps%d" % c, tag="lo%d" % c) for c in range(PACK)]
+        for c in range(PACK):
+            product(b_ps[c], xcb, z2q, c)
+
+        for c in range(PACK):
+            a4 = ring.tile([P, S], F32, name="a4")
+            a5 = ring.tile([P, S], F32, name="a5")
+            e4 = ring.tile([P, S], F32, name="e4")
+            e5 = ring.tile([P, S], F32, name="e5")
+            t1 = ring.tile([P, S], F32, name="t1")
+            t2 = ring.tile([P, S], F32, name="t2")
+            res = ring.tile([P, S], F32, name="res")
+            nc.scalar.activation(out=a_win[c][:, :S], in_=a_ps[c][:], func=COPY, scale=0.0625)
+            nc.scalar.activation(out=a5[:], in_=a_win[c][:].indirect(l_n5[:]), func=COPY)
+            nc.scalar.activation(out=a4[:], in_=a_win[c][:].indirect(l_n4[:]), func=COPY)
+            nc.scalar.activation(out=b_win[c][:, :S], in_=b_ps[c][:], func=COPY, scale=0.03125)
+            nc.vector.scalar_tensor_tensor(out=e5[:], in0=a_ps[c][:], scalar=-0.0625, in1=a5[:], op0=MULT, op1=ADD)
+            nc.vector.scalar_tensor_tensor(out=e4[:], in0=a_ps[c][:], scalar=-0.0625, in1=a4[:], op0=MULT, op1=ADD)
+            nc.vector.tensor_tensor(out=t2[:], in0=b_win[c][:].indirect(l_n6[:]), in1=e5[:], op=MULT)
+            nc.vector.scalar_tensor_tensor(out=t1[:], in0=b_ps[c][:], scalar=0.0625, in1=e4[:], op0=MULT, op1=MULT)
+            nc.vector.tensor_tensor(out=res[:], in0=t1[:], in1=t2[:], op=ADD)
+            nc.sync.dma_start(out=out[P * c : P * (c + 1), :], in_=res[:])

@@ -19,6 +19,7 @@ P = 128
 PACK = 4
 T = 2048
 S = 512
+HALF = 256
 WIDE = 1024
 NARROW = 520
 FLOPS = 3 * 2 * 512 * 512 * 512
@@ -42,6 +43,9 @@ def tile_picked_twocdflowbquadesa_none_p_kernel(tc, x_words, x_scales, w1, sl, t
             nc.gpsimd.dma_start(out=tile[:], in_=src.rearrange("(p t) o -> p (t o)", t=PACK))
             return tile
 
+        warm = keep.tile([P, 16], F32, name="warm")
+        nc.vector.memset(warm[:, 0:1], 0.0)
+        nc.scalar.activation(out=warm[:, 8:9], in_=warm[:, 0:1], func=SIGMOID)
         xw = keep.tile([P, T], U32, name="xw", align_bytes=64)
         xs = keep.tile([P, T], U8, name="xs", align_bytes=64)
         nc.vector.memset(xs[:].bitcast(I32), 0)
@@ -77,10 +81,11 @@ def tile_picked_twocdflowbquadesa_none_p_kernel(tc, x_words, x_scales, w1, sl, t
 
         def window(name, width):
             tile = keep.tile([P, width], F32, name=name, align_bytes=64)
-            nc.vector.memset(tile[:, S:], 0.0)
+            clearer = nc.vector if width == WIDE else nc.gpsimd
+            clearer.memset(tile[:, S:], 0.0)
             return tile
 
-        y_win = [window("y_win%d" % t, WIDE) for t in range(PACK)]
+        y_win = [window("y_win%d" % t, NARROW) for t in range(PACK)]
         u_win = [window("u_win%d" % t, WIDE) for t in range(PACK)]
         a_win = [window("a_win%d" % t, NARROW) for t in range(PACK)]
         b_win = [window("b_win%d" % t, NARROW) for t in range(PACK)]
@@ -93,12 +98,6 @@ def tile_picked_twocdflowbquadesa_none_p_kernel(tc, x_words, x_scales, w1, sl, t
         def pick(lst, words, scales):
             nc.vector.tensor_copy(out=words[:], in_=xw[:].indirect(lst[:]))
             nc.vector.tensor_copy(out=scales[:], in_=xs[:].indirect(lst[:]))
-            return words, scales
-
-        def quantize(grouped, name):
-            words = keep.tile([P, S], U32, name=name + "_w", align_bytes=64)
-            scales = keep.tile([P, S], U8, name=name + "_s", align_bytes=64)
-            nc.vector.quantize_mx(out=words[:].bitcast(FP8X4), scales=scales[:], in_=grouped[:])
             return words, scales
 
         def product(bank, stat, mov, i):
@@ -116,7 +115,9 @@ def tile_picked_twocdflowbquadesa_none_p_kernel(tc, x_words, x_scales, w1, sl, t
         for h in range(2):
             nc.vector.quantize_mx(out=wq[0][:, 256 * h : 256 * (h + 1)].bitcast(FP8X4), scales=wq[1][:, 256 * h : 256 * (h + 1)],
                                   in_=w_grp[:, 1024 * h : 1024 * (h + 1)])
-        xca = pick(l_ca, *mx_tiles("xca"))
+        xca_w = keep.tile([P, S], U32, name="xca_w", align_bytes=64)
+        xca_s = reuse.tile([P, S], U8, name="xca_s", align_bytes=64, offset=2560)
+        xca = pick(l_ca, xca_w, xca_s)
         xcb_w = reuse.tile([P, S], U32, name="xcb_w", align_bytes=64, offset=0)
         xcb_s = reuse.tile([P, S], U8, name="xcb_s", align_bytes=64, offset=2048)
         xcb = pick(l_cb, xcb_w, xcb_s)
@@ -134,31 +135,36 @@ def tile_picked_twocdflowbquadesa_none_p_kernel(tc, x_words, x_scales, w1, sl, t
             nc.scalar.activation(out=u_win[t][:, :S], in_=y_ps[t][:], func=COPY, scale=zfac[:, t : t + 1])
             nc.sync.dma_start(out=u_dup[t][:], in_=u_win[t][:, :S])
         for t in range(PACK):
-            nc.vector.tensor_scalar(out=ry[:, t, :], in0=y_ps[t][:], scalar1=gs2_t[:, t : t + 1], scalar2=None, op0=MULT)
-        for t in range(PACK):
             nc.scalar.copy(out=y_win[t][:, :S], in_=y_ps[t][:])
             nc.scalar.activation(out=g1[t][:], in_=y_win[t][:].indirect(l_n1[:]), func=COPY)
             nc.vector.tensor_tensor(out=d2[:, t, :], in0=u_win[t][:].indirect(l_n2[:]), in1=u_dup[t][:], op=SUB)
             nc.vector.tensor_tensor(out=d1[:, t, :], in0=g1[t][:], in1=y_ps[t][:], op=SUB)
+            nc.gpsimd.tensor_scalar(out=ry[:, t, :], in0=y_win[t][:, :S], scalar1=gs2_t[:, t : t + 1], scalar2=0.0, op0=MULT, op1=ADD)
 
-        def weave(f0, f1, name):
-            grouped = keep.tile([P, PACK * S], BF16, name=name, tag="grouped", align_bytes=64)
-            nc.vector.tensor_tensor(out=grouped[:].rearrange("p (c i t) -> p c t i", i=2, t=PACK),
-                                    in0=f0[:].rearrange("p t (c i) -> p c t i", i=2),
-                                    in1=f1[:].rearrange("p t (c i) -> p c t i", i=2), op=MULT)
-            return grouped
+        def score(f0, f1, stat, name, bank_tag):
+            words, scales = mx_tiles(name)
+            banks = [psum.tile([P, S], F32, name="%s_ps%d" % (name, c), tag="%s%d" % (bank_tag, c)) for c in range(PACK)]
+            halves = [slice(HALF * h, HALF * (h + 1)) for h in range(2)]
+            grouped = [keep.tile([P, PACK * HALF], BF16, name="%s_grp%d" % (name, h), tag="grouped%d" % h, align_bytes=64) for h in range(2)]
+            for h in range(2):
+                nc.vector.tensor_tensor(out=grouped[h][:].rearrange("p (c i t) -> p c t i", i=2, t=PACK),
+                                        in0=f0[:, :, halves[h]].rearrange("p t (c i) -> p c t i", i=2),
+                                        in1=f1[:, :, halves[h]].rearrange("p t (c i) -> p c t i", i=2), op=MULT)
+            for h in range(2):
+                nc.vector.quantize_mx(out=words[:, halves[h]].bitcast(FP8X4), scales=scales[:, halves[h]], in_=grouped[h][:])
+            for c in range(PACK):
+                rows = slice(P * c, P * (c + 1))
+                for h in range(2):
+                    nc.tensor.matmul_mx(out=banks[c][:, halves[h]], lhsT=stat[0][:, rows].bitcast(FP8X4), lhsT_scale=stat[1][:, rows],
+                                        rhs=words[:, halves[h]].bitcast(FP8X4), rhs_scale=scales[:, halves[h]], start=True, stop=True)
+            return banks
 
-        zq = quantize(weave(d1, d2, "z_grp"), "zq")
-        a_ps = [psum.tile([P, S], F32, name="a_ps%d" % c, tag="hi%d" % c) for c in range(PACK)]
-        for c in range(PACK):
-            product(a_ps[c], xca, zq, c)
+        a_ps = score(d1, d2, xca, "z", "hi")
         for t in range(PACK):
-            nc.scalar.activation(out=sg[:, t, :], in_=y_win[t][:].indirect(l_n3[:]), func=SIGMOID,
-                                 bias=sbias[:, t : t + 1], scale=sl_t[:, t : t + 1])
-        z2q = quantize(weave(ry, sg, "z2_grp"), "z2q")
-        b_ps = [psum.tile([P, S], F32, name="b_ps%d" % c, tag="lo%d" % c) for c in range(PACK)]
-        for c in range(PACK):
-            product(b_ps[c], xcb, z2q, c)
+            for h in range(2):
+                nc.scalar.activation(out=sg[:, t, HALF * h : HALF * (h + 1)], in_=y_win[t][:].indirect(l_n3[:, 16 * h : 16 * (h + 1)]), func=SIGMOID,
+                                     bias=sbias[:, t : t + 1], scale=sl_t[:, t : t + 1])
+        b_ps = score(ry, sg, xcb, "z2", "lo")
 
         for c in range(PACK):
             a4 = ring.tile([P, S], F32, name="a4")
@@ -169,12 +175,20 @@ def tile_picked_twocdflowbquadesa_none_p_kernel(tc, x_words, x_scales, w1, sl, t
             t2 = ring.tile([P, S], F32, name="t2")
             res = ring.tile([P, S], F32, name="res")
             nc.scalar.activation(out=a_win[c][:, :S], in_=a_ps[c][:], func=COPY, scale=0.0625)
+            if c == 0:
+                nc.vector.tensor_scalar(out=b_win[c][:, :S], in0=b_ps[c][:], scalar1=0.03125, scalar2=None, op0=MULT)
+            else:
+                nc.scalar.activation(out=b_win[c][:, :S], in_=b_ps[c][:], func=COPY, scale=0.03125)
             nc.scalar.activation(out=a5[:], in_=a_win[c][:].indirect(l_n5[:]), func=COPY)
             nc.scalar.activation(out=a4[:], in_=a_win[c][:].indirect(l_n4[:]), func=COPY)
-            nc.scalar.activation(out=b_win[c][:, :S], in_=b_ps[c][:], func=COPY, scale=0.03125)
             nc.vector.scalar_tensor_tensor(out=e5[:], in0=a_ps[c][:], scalar=-0.0625, in1=a5[:], op0=MULT, op1=ADD)
             nc.vector.scalar_tensor_tensor(out=e4[:], in0=a_ps[c][:], scalar=-0.0625, in1=a4[:], op0=MULT, op1=ADD)
             nc.vector.tensor_tensor(out=t2[:], in0=b_win[c][:].indirect(l_n6[:]), in1=e5[:], op=MULT)
-            nc.vector.scalar_tensor_tensor(out=t1[:], in0=b_ps[c][:], scalar=0.0625, in1=e4[:], op0=MULT, op1=MULT)
-            nc.vector.tensor_tensor(out=res[:], in0=t1[:], in1=t2[:], op=ADD)
-            nc.sync.dma_start(out=out[P * c : P * (c + 1), :], in_=res[:])
+            last = c == PACK - 1
+            parts = [slice(0, HALF), slice(HALF, S)] if last else [slice(0, S)]
+            adder = nc.vector if last else nc.gpsimd
+            for cols in parts:
+                nc.vector.scalar_tensor_tensor(out=t1[:, cols], in0=b_ps[c][:, cols], scalar=0.0625, in1=e4[:, cols], op0=MULT, op1=MULT)
+            for cols in parts:
+                adder.tensor_tensor(out=res[:, cols], in0=t1[:, cols], in1=t2[:, cols], op=ADD)
+                nc.sync.dma_start(out=out[P * c : P * (c + 1), cols], in_=res[:, cols])

from contextlib import ExitStack

import concourse.mybir as mybir

F32 = mybir.dt.float32
BF16 = mybir.dt.bfloat16
I32 = mybir.dt.int32
U32 = mybir.dt.uint32
U16 = mybir.dt.uint16
U8 = mybir.dt.uint8
FP8X4 = mybir.dt.float8_e4m3fn_x4
MULT = mybir.AluOpType.mult
ADD = mybir.AluOpType.add
SUB = mybir.AluOpType.subtract
COPY = mybir.ActivationFunctionType.Copy
SIGMOID = mybir.ActivationFunctionType.Sigmoid

P = 128
PACK = 4
T = 2048
S = 512
HALF = 256
WIDE = 1024
NARROW = 520
FLOPS = 3 * 2 * 512 * 512 * 512


def tile_picked_twocdflowbquadesa_none_p_kernel(tc, x_words, x_scales, w1, sl, th, gs, gs2, offs, n1, n2, n3, ca, cb, n4, n5, n6, out):
    nc = tc.nc
    with ExitStack() as ctx:
        keep = ctx.enter_context(tc.tile_pool(name="keep", bufs=1))
        ring = ctx.enter_context(tc.tile_pool(name="ring", bufs=3))
        reuse = ctx.enter_context(tc.tile_pool(name="reuse", bufs=1))
        psum = ctx.enter_context(tc.psum_pool(name="psum", bufs=1))

        def load_list(src, name):
            tile = keep.tile([P, S // 16], U16, name=name)
            nc.sync.dma_start(out=tile[:], in_=src)
            return tile

        def load_rows(src, name):
            tile = keep.tile([P, PACK], F32, name=name)
            nc.gpsimd.dma_start(out=tile[:], in_=src.rearrange("(p t) o -> p (t o)", t=PACK))
            return tile

        warm = keep.tile([P, 16], F32, name="warm")
        nc.vector.memset(warm[:, 0:1], 0.0)
        nc.scalar.activation(out=warm[:, 8:9], in_=warm[:, 0:1], func=SIGMOID)
        xw = keep.tile([P, T], U32, name="xw", align_bytes=64)
        xs = keep.tile([P, T], U8, name="xs", align_bytes=64)
        nc.vector.memset(xs[:].bitcast(I32), 0)
        nc.sync.dma_start(out=xw[:].bitcast(I32), in_=x_words[0].rearrange("p n t -> p (n t)").bitcast(I32))
        l_offs = load_list(offs, "l_offs")
        for q in range(4):
            nc.sync.dma_start(out=xs[32 * q : 32 * q + 4, :].bitcast(I32), in_=x_scales[0, 4 * q : 4 * q + 4, :].bitcast(I32))
        w_rows = w1.rearrange("(p j) c -> p j c", j=PACK)
        w_raw = []
        for h in range(2):
            tile = keep.tile([P, PACK, 256], F32, name="w_raw%d" % h)
            nc.sync.dma_start(out=tile[:], in_=w_rows[:, :, 256 * h : 256 * (h + 1)])
            w_raw.append(tile)
        l_ca = load_list(ca, "l_ca")
        l_cb = load_list(cb, "l_cb")
        l_n1 = load_list(n1, "l_n1")
        l_n2 = load_list(n2, "l_n2")
        l_n3 = load_list(n3, "l_n3")
        l_n5 = load_list(n5, "l_n5")
        l_n4 = load_list(n4, "l_n4")
        l_n6 = load_list(n6, "l_n6")

        gs_t = load_rows(gs, "gs_t")
        gs2_t = load_rows(gs2, "gs2_t")
        sl_t = load_rows(sl, "sl_t")
        th_t = load_rows(th, "th_t")
        zfac = keep.tile([P, PACK], F32, name="zfac")
        nc.gpsimd.tensor_scalar(out=zfac[:], in0=gs_t[:], scalar1=0.75, scalar2=0.0, op0=MULT, op1=ADD)
        nth = keep.tile([P, PACK], F32, name="nth")
        nc.gpsimd.tensor_scalar(out=nth[:], in0=th_t[:], scalar1=-1.0, scalar2=0.0, op0=MULT, op1=ADD)
        sbias = keep.tile([P, PACK], F32, name="sbias")
        nc.gpsimd.tensor_tensor(out=sbias[:], in0=nth[:], in1=sl_t[:], op=MULT)

        def window(name, width):
            tile = keep.tile([P, width], F32, name=name, align_bytes=64)
            clearer = nc.vector if width == WIDE else nc.gpsimd
            clearer.memset(tile[:, S:], 0.0)
            return tile

        y_win = [window("y_win%d" % t, NARROW) for t in range(PACK)]
        u_win = [window("u_win%d" % t, WIDE) for t in range(PACK)]
        a_win = [window("a_win%d" % t, NARROW) for t in range(PACK)]
        b_win = [window("b_win%d" % t, NARROW) for t in range(PACK)]

        def mx_tiles(name):
            words = keep.tile([P, S], U32, name=name + "_w", align_bytes=64)
            scales = keep.tile([P, S], U8, name=name + "_s", align_bytes=64)
            return words, scales

        def pick(lst, words, scales):
            nc.vector.tensor_copy(out=words[:], in_=xw[:].indirect(lst[:]))
            nc.vector.tensor_copy(out=scales[:], in_=xs[:].indirect(lst[:]))
            return words, scales

        def product(bank, stat, mov, i):
            cols = slice(P * i, P * (i + 1))
            nc.tensor.matmul_mx(out=bank[:], lhsT=stat[0][:, cols].bitcast(FP8X4), lhsT_scale=stat[1][:, cols],
                                rhs=mov[0][:].bitcast(FP8X4), rhs_scale=mov[1][:], start=True, stop=True)

        xq = pick(l_offs, *mx_tiles("xq"))

        w_grp = reuse.tile([P, PACK * S], BF16, name="w_grp", align_bytes=64, offset=0)
        w_view = w_grp[:].rearrange("p (t m j) -> p m t j", t=PACK, j=PACK)
        for h in range(2):
            nc.scalar.copy(out=w_view[:, 64 * h : 64 * (h + 1), :, :], in_=w_raw[h][:].rearrange("p j (m t) -> p m t j", t=PACK))
        wq = mx_tiles("wq")
        for h in range(2):
            nc.vector.quantize_mx(out=wq[0][:, 256 * h : 256 * (h + 1)].bitcast(FP8X4), scales=wq[1][:, 256 * h : 256 * (h + 1)],
                                  in_=w_grp[:, 1024 * h : 1024 * (h + 1)])
        xca_w = keep.tile([P, S], U32, name="xca_w", align_bytes=64)
        xca_s = reuse.tile([P, S], U8, name="xca_s", align_bytes=64, offset=2560)
        xca = pick(l_ca, xca_w, xca_s)
        xcb_w = reuse.tile([P, S], U32, name="xcb_w", align_bytes=64, offset=0)
        xcb_s = reuse.tile([P, S], U8, name="xcb_s", align_bytes=64, offset=2048)
        xcb = pick(l_cb, xcb_w, xcb_s)

        y_ps = [psum.tile([P, S], F32, name="y_ps%d" % t, tag="lo%d" % t) for t in range(PACK)]
        u_dup = [keep.tile([P, S], F32, name="u_dup%d" % t) for t in range(PACK)]
        g1 = [keep.tile([P, S], F32, name="g1_%d" % t) for t in range(PACK)]
        d1 = keep.tile([P, PACK, S], F32, name="d1", align_bytes=64)
        d2 = keep.tile([P, PACK, S], F32, name="d2", align_bytes=64)
        ry = keep.tile([P, PACK, S], F32, name="ry", align_bytes=64)
        sg = keep.tile([P, PACK, S], F32, name="sg", align_bytes=64)
        for t in range(PACK):
            product(y_ps[t], wq, xq, t)
        for t in range(PACK):
            nc.scalar.activation(out=u_win[t][:, :S], in_=y_ps[t][:], func=COPY, scale=zfac[:, t : t + 1])
            nc.sync.dma_start(out=u_dup[t][:], in_=u_win[t][:, :S])
        for t in range(PACK):
            nc.scalar.copy(out=y_win[t][:, :S], in_=y_ps[t][:])
            nc.scalar.activation(out=g1[t][:], in_=y_win[t][:].indirect(l_n1[:]), func=COPY)
            nc.vector.tensor_tensor(out=d2[:, t, :], in0=u_win[t][:].indirect(l_n2[:]), in1=u_dup[t][:], op=SUB)
            nc.vector.tensor_tensor(out=d1[:, t, :], in0=g1[t][:], in1=y_ps[t][:], op=SUB)
            nc.gpsimd.tensor_scalar(out=ry[:, t, :], in0=y_win[t][:, :S], scalar1=gs2_t[:, t : t + 1], scalar2=0.0, op0=MULT, op1=ADD)

        def score(f0, f1, stat, name, bank_tag):
            words, scales = mx_tiles(name)
            banks = [psum.tile([P, S], F32, name="%s_ps%d" % (name, c), tag="%s%d" % (bank_tag, c)) for c in range(PACK)]
            halves = [slice(HALF * h, HALF * (h + 1)) for h in range(2)]
            grouped = [keep.tile([P, PACK * HALF], BF16, name="%s_grp%d" % (name, h), tag="grouped%d" % h, align_bytes=64) for h in range(2)]
            for h in range(2):
                nc.vector.tensor_tensor(out=grouped[h][:].rearrange("p (c i t) -> p c t i", i=2, t=PACK),
                                        in0=f0[:, :, halves[h]].rearrange("p t (c i) -> p c t i", i=2),
                                        in1=f1[:, :, halves[h]].rearrange("p t (c i) -> p c t i", i=2), op=MULT)
            for h in range(2):
                nc.vector.quantize_mx(out=words[:, halves[h]].bitcast(FP8X4), scales=scales[:, halves[h]], in_=grouped[h][:])
            for c in range(PACK):
                rows = slice(P * c, P * (c + 1))
                for h in range(2):
                    nc.tensor.matmul_mx(out=banks[c][:, halves[h]], lhsT=stat[0][:, rows].bitcast(FP8X4), lhsT_scale=stat[1][:, rows],
                                        rhs=words[:, halves[h]].bitcast(FP8X4), rhs_scale=scales[:, halves[h]], start=True, stop=True)
            return banks

        a_ps = score(d1, d2, xca, "z", "hi")
        for t in range(PACK):
            for h in range(2):
                nc.scalar.activation(out=sg[:, t, HALF * h : HALF * (h + 1)], in_=y_win[t][:].indirect(l_n3[:, 16 * h : 16 * (h + 1)]), func=SIGMOID,
                                     bias=sbias[:, t : t + 1], scale=sl_t[:, t : t + 1])
        b_ps = score(ry, sg, xcb, "z2", "lo")

        for c in range(PACK):
            a4 = ring.tile([P, S], F32, name="a4")
            a5 = ring.tile([P, S], F32, name="a5")
            e4 = ring.tile([P, S], F32, name="e4")
            e5 = ring.tile([P, S], F32, name="e5")
            t1 = ring.tile([P, S], F32, name="t1")
            t2 = ring.tile([P, S], F32, name="t2")
            res = ring.tile([P, S], F32, name="res")
            nc.scalar.activation(out=a_win[c][:, :S], in_=a_ps[c][:], func=COPY, scale=0.0625)
            if c == 0:
                nc.vector.tensor_scalar(out=b_win[c][:, :S], in0=b_ps[c][:], scalar1=0.03125, scalar2=None, op0=MULT)
            else:
                nc.scalar.activation(out=b_win[c][:, :S], in_=b_ps[c][:], func=COPY, scale=0.03125)
            nc.scalar.activation(out=a5[:], in_=a_win[c][:].indirect(l_n5[:]), func=COPY)
            nc.scalar.activation(out=a4[:], in_=a_win[c][:].indirect(l_n4[:]), func=COPY)
            nc.vector.scalar_tensor_tensor(out=e5[:], in0=a_ps[c][:], scalar=-0.0625, in1=a5[:], op0=MULT, op1=ADD)
            nc.vector.scalar_tensor_tensor(out=e4[:], in0=a_ps[c][:], scalar=-0.0625, in1=a4[:], op0=MULT, op1=ADD)
            nc.vector.tensor_tensor(out=t2[:], in0=b_win[c][:].indirect(l_n6[:]), in1=e5[:], op=MULT)
            last = c == PACK - 1
            parts = [slice(0, HALF), slice(HALF, S)] if last else [slice(0, S)]
            adder = nc.vector if last else nc.gpsimd
            for cols in parts:
                nc.vector.scalar_tensor_tensor(out=t1[:, cols], in0=b_ps[c][:, cols], scalar=0.0625, in1=e4[:, cols], op0=MULT, op1=MULT)
            for cols in parts:
                adder.tensor_tensor(out=res[:, cols], in0=t1[:, cols], in1=t2[:, cols], op=ADD)
                nc.sync.dma_start(out=out[P * c : P * (c + 1), cols], in_=res[:, cols])
